import numpy as np
import ml_dtypes


def mxq(x, axis, fmt="e4m3"):
    dtype, down = {"e4m3": (ml_dtypes.float8_e4m3fn, 7), "e5m2": (ml_dtypes.float8_e5m2, 14)}[fmt]
    v = np.moveaxis(np.asarray(x, np.float32).astype(ml_dtypes.bfloat16).astype(np.float64), axis, -1)
    blocks = v.reshape(v.shape[:-1] + (-1, 32))
    amax = np.abs(blocks).max(-1, keepdims=True)
    byte = np.maximum(np.where(amax > 0, np.frexp(amax)[1] - 1 + 127, 0) - down, 1)
    scale = np.exp2(byte - 127.0)
    codes = (blocks / scale).astype(np.float32).astype(dtype).astype(np.float64)
    return np.moveaxis((codes * scale).reshape(v.shape), -1, axis)


WIDE = False


def mx_kscale(k):
    if not WIDE:
        return np.ones(k)
    levels = np.array([10, -10, 5, -5, 0])
    if k % 512:
        return np.exp2(np.random.permutation(np.resize(levels, k // 32))).repeat(32)
    a = np.empty((k // 512, 16))
    for p in range(k // 512):
        a[p, :8] = np.random.permutation(np.resize(levels, 8))
        for g in range(8):
            far = levels[np.abs(levels - a[p, g]) >= 10]
            a[p, g + 8] = far[np.random.randint(len(far))]
    return np.exp2(a.ravel()).repeat(32)


def f64(x):
    return np.asarray(x).astype(np.float64)


def striped(idx):
    return np.tile(np.asarray(idx).reshape(-1, 16).T, (8, 1)).astype(np.uint16)


def unstriped(offs):
    return offs[:16].T.reshape(-1).astype(np.int64)


E2M1 = np.array([0.0, 0.5, 1.0, 1.5, 2.0, 3.0, 4.0, 6.0, -0.0, -0.5, -1.0, -1.5, -2.0, -3.0, -4.0, -6.0])


def pack_weight(w, fmt):
    k, n = w.shape
    w = f64(np.asarray(w, np.float32).astype(ml_dtypes.bfloat16)).reshape(k // 32, 32, n)
    amax = np.abs(w).max(1)
    if fmt == "e4m3":
        byte = np.frexp(amax)[1] - 1 + 127 - 7
    else:
        mant, ex = np.frexp(amax / 6.0)
        byte = np.where(mant > 0.5, ex, ex - 1) + 127
    byte = np.clip(np.where(amax > 0, byte, 1), 1, 254)
    scaled = (w * np.exp2(127.0 - byte)[:, None, :]).reshape(k, n).astype(np.float32)
    by_word = np.ascontiguousarray(scaled.reshape(k // 512, 128, 4, n).transpose(0, 1, 3, 2))
    if fmt == "e4m3":
        words = by_word.astype(ml_dtypes.float8_e4m3fn).view(np.uint8)
    else:
        c = by_word.astype(ml_dtypes.float4_e2m1fn).view(np.uint8) & 0xF
        words = (c[..., 0::2] | (c[..., 1::2] << 4)).reshape(k // 512, 128, 2 * n)
    return np.ascontiguousarray(words), np.ascontiguousarray(byte.astype(np.uint8).reshape(k // 512, 16, n))


def unpack_weight(words, scales, fmt):
    g, _, n = scales.shape
    words = np.ascontiguousarray(words).reshape(g, 128, n, -1)
    if fmt == "e4m3":
        vals = words.view(ml_dtypes.float8_e4m3fn).astype(np.float64)
    else:
        nib = np.empty((g, 128, n, 4), np.uint8)
        nib[..., 0::2] = words & 0xF
        nib[..., 1::2] = words >> 4
        vals = E2M1[nib]
    vals = vals * np.repeat(np.exp2(scales.astype(np.float64) - 127.0), 8, axis=1)[..., None]
    return vals.transpose(0, 1, 3, 2).reshape(g * 512, n)


D, T, I, J, U, M, N = 512, 2048, 512, 512, 1024, 512, 64


def setup_inputs():
    n = np.random.standard_normal
    idx = np.random.permutation(T)[:I]
    idx2 = np.random.permutation(U)[:J]
    idx3 = np.random.permutation(M)[:N]
    fd = mx_kscale(D)
    keysp = pack_weight(n((D, T)) / fd[:, None], "e4m3")
    return {
        "keys_words": keysp[0],
        "keys_scales": keysp[1],
        "notes": (n((D, U)) * 1.0 / np.sqrt(D) * fd[:, None]).astype(np.float32),
        "old": (1.0 * n((I, M))).astype(np.float32),
        "offs": striped(idx),
        "offs2": striped(idx2),
        "offs3": striped(idx3),
    }


def reference(keys_words, keys_scales, notes, old, offs, offs2, offs3):
    idx = unstriped(offs)
    idx2 = unstriped(offs2)
    idx3 = unstriped(offs3)
    keysu = unpack_weight(keys_words, keys_scales, "e4m3")
    keysidxg = keysu[:, idx]
    notesidx2q = mxq(f64(notes)[:, idx2], 0, "e4m3")
    g0 = keysidxg.T @ notesidx2q
    rb0 = g0.reshape(I, N, J // N).max(axis=2)
    gf = np.zeros((I, M))
    gf[:, idx3] = rb0
    y = f64(old) + gf
    return y

@@ -1,0 +1,141 @@
+from contextlib import ExitStack
+
+import concourse.mybir as mybir
+
+F32 = mybir.dt.float32
+BF16 = mybir.dt.bfloat16
+I32 = mybir.dt.int32
+U32 = mybir.dt.uint32
+U16 = mybir.dt.uint16
+U8 = mybir.dt.uint8
+FP8X4 = mybir.dt.float8_e4m3fn_x4
+COPY = mybir.ActivationFunctionType.Copy
+ADD = mybir.AluOpType.add
+MAX = mybir.AluOpType.max
+AXIS_X = mybir.AxisListType.X
+
+P = 128
+D, T, I, J, U, M, N = 512, 2048, 512, 512, 1024, 512, 64
+PACK = 4
+RUN = J // N
+ROW_TILES = I // P
+FLOPS = 2 * D * I * J
+
+
+def tile_attend_tab_plain_runsput_kernel(tc, keys_words, keys_scales, notes, old, offs, offs2, offs3, out):
+    nc = tc.nc
+    with ExitStack() as ctx:
+        lists = ctx.enter_context(tc.tile_pool(name="lists", bufs=1))
+        sb = ctx.enter_context(tc.tile_pool(name="sb", bufs=1))
+        psum = ctx.enter_context(tc.psum_pool(name="psum", bufs=1))
+
+        key_list = lists.tile([P, I // 16], U16, name="key_list")
+        note_list = lists.tile([P, J // 16], U16, name="note_list")
+        run_list = lists.tile([P, N // 16], U16, name="run_list")
+
+        planes = [sb.tile([P, U], F32, name="plane%d" % t) for t in range(PACK)]
+        pool_words = sb.tile([P, T], I32, name="pool_words")
+        pool_scales = sb.tile([P, T], U8, name="pool_scales")
+        old_tiles = [sb.tile([P, M], F32, name="old%d" % r) for r in range(ROW_TILES)]
+        placed = [sb.tile([P, M], F32, name="placed%d" % r) for r in range(ROW_TILES)]
+
+        nc.vector.memset(pool_scales[:].bitcast(I32), 0)
+
+        notes_by_plane = notes.rearrange("(p t) u -> t p u", t=PACK)
+        nc.sync.dma_start(note_list[:], offs2)
+        nc.sync.dma_start(key_list[:], offs)
+        nc.sync.dma_start(out=planes[0][:], in_=notes_by_plane[0])
+        for q in range(4):
+            nc.sync.dma_start(
+                out=pool_scales[32 * q : 32 * q + 4, :].bitcast(I32),
+                in_=keys_scales[0, 4 * q : 4 * q + 4, :].bitcast(I32),
+            )
+        for t in range(1, PACK):
+            nc.sync.dma_start(out=planes[t][:], in_=notes_by_plane[t])
+        nc.sync.dma_start(out=pool_words[:], in_=keys_words[0].rearrange("p c r -> p (c r)").bitcast(I32))
+        nc.sync.dma_start(run_list[:], offs3)
+        for r in range(ROW_TILES):
+            nc.sync.dma_start(out=old_tiles[r][:], in_=old[r * P : (r + 1) * P, :])
+
+        for r in range(ROW_TILES):
+            engine = nc.vector if r < 2 else nc.gpsimd
+            engine.memset(placed[r][:], 0.0)
+
+        picked = sb.tile([P, PACK, J], BF16, name="picked")
+        key_scales = sb.tile([P, I], U8, name="key_scales", align_bytes=64)
+
+        def gather_notes(engine, t, lo, hi):
+            window = planes[t][:].indirect(note_list[:, lo // 16 : hi // 16])
+            if engine is nc.vector:
+                nc.vector.tensor_copy(picked[:, t, lo:hi], window)
+            else:
+                nc.scalar.activation(picked[:, t, lo:hi], window, COPY)
+
+        half = J // 2
+        woven = [sb.tile([P, half, PACK], BF16, name="woven%d" % h, align_bytes=64) for h in range(2)]
+
+        def weave(engine, h, first_plane):
+            pair = slice(first_plane, first_plane + 2)
+            dst = woven[h][:, :, pair].rearrange("p (c i) t -> p c t i", i=4)
+            src = picked[:, pair, h * half : (h + 1) * half].rearrange("p t (c i) -> p c t i", i=4)
+            if engine is nc.vector:
+                nc.vector.tensor_copy(dst, src)
+            else:
+                nc.scalar.copy(dst, src)
+
+        note_codes = sb.tile([P, J], U32, name="note_codes", align_bytes=64)
+        note_scales = sb.tile([P, J], U8, name="note_scales", align_bytes=64)
+
+        def quantise(h):
+            cols = slice(h * half, (h + 1) * half)
+            nc.vector.quantize_mx(
+                out=note_codes[:, cols].bitcast(FP8X4),
+                scales=note_scales[:, cols],
+                in_=woven[h][:].rearrange("p c t -> p (c t)"),
+            )
+
+        nc.vector.tensor_copy(key_scales[:], pool_scales[:].indirect(key_list[:]))
+        gather_notes(nc.scalar, 0, 0, J)
+        gather_notes(nc.vector, 1, 0, 320)
+        gather_notes(nc.scalar, 1, 320, J)
+        weave(nc.scalar, 0, 0)
+        weave(nc.scalar, 1, 0)
+        gather_notes(nc.vector, 2, 0, J)
+        gather_notes(nc.vector, 3, 0, 320)
+        gather_notes(nc.scalar, 3, 320, J)
+        weave(nc.vector, 0, 2)
+        weave(nc.scalar, 1, 2)
+        quantise(0)
+        quantise(1)
+
+        key_words = [sb.tile([P, P], U32, name="key_words%d" % r, align_bytes=64) for r in range(ROW_TILES)]
+        word_window = pool_words[:].bitcast(U32)
+        for r in range(ROW_TILES):
+            nc.vector.tensor_copy(key_words[r][:], word_window.indirect(key_list[:, r * P // 16 : (r + 1) * P // 16]))
+
+        banks = [psum.tile([P, J], F32, name="bank%d" % r) for r in range(ROW_TILES)]
+        largest = [sb.tile([P, N], F32, name="largest%d" % r) for r in range(ROW_TILES)]
+        for r in range(ROW_TILES):
+            nc.tensor.matmul_mx(
+                out=banks[r][:],
+                lhsT=key_words[r][:].bitcast(FP8X4),
+                lhsT_scale=key_scales[:, r * P : (r + 1) * P],
+                rhs=note_codes[:].bitcast(FP8X4),
+                rhs_scale=note_scales[:],
+                start=True,
+                stop=True,
+            )
+            nc.vector.tensor_reduce(
+                out=largest[r][:],
+                in_=banks[r][:].rearrange("p (n e) -> p n e", e=RUN),
+                axis=AXIS_X,
+                op=MAX,
+            )
+            nc.scalar.activation(placed[r][:].indirect(run_list[:]), largest[r][:], COPY)
+
+        pieces = [(r, 0, M) for r in range(ROW_TILES - 1)] + [(ROW_TILES - 1, 0, M // 2), (ROW_TILES - 1, M // 2, M)]
+        for r, lo, hi in pieces:
+            result = sb.tile([P, hi - lo], F32, name="result%d_%d" % (r, lo))
+            engine = nc.gpsimd if r == 0 else nc.vector
+            engine.tensor_tensor(result[:], old_tiles[r][:, lo:hi], placed[r][:, lo:hi], ADD)
+            nc.sync.dma_start(out=out[r * P : (r + 1) * P, lo:hi], in_=result[:])

@@ -41,6 +41,11 @@ def tile_attend_tab_plain_runsput_kernel(tc, keys_words, keys_scales, notes, old
 
         nc.vector.memset(pool_scales[:].bitcast(I32), 0)
 
+        warm_in = sb.tile([P, 1], F32, name="warm_in")
+        warm_out = sb.tile([P, 1], F32, name="warm_out")
+        nc.gpsimd.memset(warm_in[:], 0.0)
+        nc.scalar.activation(warm_out[:], warm_in[:], COPY)
+
         notes_by_plane = notes.rearrange("(p t) u -> t p u", t=PACK)
         nc.sync.dma_start(note_list[:], offs2)
         nc.sync.dma_start(key_list[:], offs)

@@ -41,19 +41,14 @@ def tile_attend_tab_plain_runsput_kernel(tc, keys_words, keys_scales, notes, old
 
         nc.vector.memset(pool_scales[:].bitcast(I32), 0)
 
-        warm_in = sb.tile([P, 1], F32, name="warm_in")
-        warm_out = sb.tile([P, 1], F32, name="warm_out")
-        nc.gpsimd.memset(warm_in[:], 0.0)
-        nc.scalar.activation(warm_out[:], warm_in[:], COPY)
-
         notes_by_plane = notes.rearrange("(p t) u -> t p u", t=PACK)
         nc.sync.dma_start(note_list[:], offs2)
         nc.sync.dma_start(key_list[:], offs)
         nc.sync.dma_start(out=planes[0][:], in_=notes_by_plane[0])
         for q in range(4):
             nc.sync.dma_start(
-                out=pool_scales[32 * q : 32 * q + 4, :].bitcast(I32),
-                in_=keys_scales[0, 4 * q : 4 * q + 4, :].bitcast(I32),
+                out=pool_scales[q:P:32, :].bitcast(I32),
+                in_=keys_scales[0, q:16:4, :].bitcast(I32),
             )
         for t in range(1, PACK):
             nc.sync.dma_start(out=planes[t][:], in_=notes_by_plane[t])
@@ -77,12 +72,11 @@ def tile_attend_tab_plain_runsput_kernel(tc, keys_words, keys_scales, notes, old
                 nc.scalar.activation(picked[:, t, lo:hi], window, COPY)
 
         half = J // 2
-        woven = [sb.tile([P, half, PACK], BF16, name="woven%d" % h, align_bytes=64) for h in range(2)]
+        woven = [sb.tile([P, half, PACK], BF16, name="woven%d" % h, tag="woven%d" % h, align_bytes=64) for h in range(2)]
 
-        def weave(engine, h, first_plane):
-            pair = slice(first_plane, first_plane + 2)
-            dst = woven[h][:, :, pair].rearrange("p (c i) t -> p c t i", i=4)
-            src = picked[:, pair, h * half : (h + 1) * half].rearrange("p t (c i) -> p c t i", i=4)
+        def weave(engine, h, lo, hi):
+            dst = woven[h][:, lo - h * half : hi - h * half, :].rearrange("p (c i) t -> p c t i", i=4)
+            src = picked[:, :, lo:hi].rearrange("p t (c i) -> p c t i", i=4)
             if engine is nc.vector:
                 nc.vector.tensor_copy(dst, src)
             else:
@@ -101,30 +95,34 @@ def tile_attend_tab_plain_runsput_kernel(tc, keys_words, keys_scales, notes, old
 
         nc.vector.tensor_copy(key_scales[:], pool_scales[:].indirect(key_list[:]))
         gather_notes(nc.scalar, 0, 0, J)
-        gather_notes(nc.vector, 1, 0, 320)
-        gather_notes(nc.scalar, 1, 320, J)
-        weave(nc.scalar, 0, 0)
-        weave(nc.scalar, 1, 0)
-        gather_notes(nc.vector, 2, 0, J)
+        gather_notes(nc.vector, 1, 0, J)
+        gather_notes(nc.vector, 2, 0, half)
+        gather_notes(nc.scalar, 2, half, J)
         gather_notes(nc.vector, 3, 0, 320)
         gather_notes(nc.scalar, 3, 320, J)
-        weave(nc.vector, 0, 2)
-        weave(nc.scalar, 1, 2)
-        quantise(0)
+        weave(nc.scalar, 1, 320, J)
+        weave(nc.vector, 1, half, 320)
+        weave(nc.vector, 0, 0, half)
         quantise(1)
+        quantise(0)
 
-        key_words = [sb.tile([P, P], U32, name="key_words%d" % r, align_bytes=64) for r in range(ROW_TILES)]
+        key_words = sb.tile([P, I], U32, name="key_words", tag="woven1", align_bytes=64)
         word_window = pool_words[:].bitcast(U32)
         for r in range(ROW_TILES):
-            nc.vector.tensor_copy(key_words[r][:], word_window.indirect(key_list[:, r * P // 16 : (r + 1) * P // 16]))
+            nc.vector.tensor_copy(
+                key_words[:, r * P : (r + 1) * P],
+                word_window.indirect(key_list[:, r * P // 16 : (r + 1) * P // 16]),
+            )
 
         banks = [psum.tile([P, J], F32, name="bank%d" % r) for r in range(ROW_TILES)]
         largest = [sb.tile([P, N], F32, name="largest%d" % r) for r in range(ROW_TILES)]
-        for r in range(ROW_TILES):
+
+        def place_largest(r):
+            rows = slice(r * P, (r + 1) * P)
             nc.tensor.matmul_mx(
                 out=banks[r][:],
-                lhsT=key_words[r][:].bitcast(FP8X4),
-                lhsT_scale=key_scales[:, r * P : (r + 1) * P],
+                lhsT=key_words[:, rows].bitcast(FP8X4),
+                lhsT_scale=key_scales[:, rows],
                 rhs=note_codes[:].bitcast(FP8X4),
                 rhs_scale=note_scales[:],
                 start=True,
@@ -138,9 +136,17 @@ def tile_attend_tab_plain_runsput_kernel(tc, keys_words, keys_scales, notes, old
             )
             nc.scalar.activation(placed[r][:].indirect(run_list[:]), largest[r][:], COPY)
 
-        pieces = [(r, 0, M) for r in range(ROW_TILES - 1)] + [(ROW_TILES - 1, 0, M // 2), (ROW_TILES - 1, M // 2, M)]
-        for r, lo, hi in pieces:
+        def add_and_store(r, shares):
+            lo, hi = shares[0][1], shares[-1][2]
             result = sb.tile([P, hi - lo], F32, name="result%d_%d" % (r, lo))
-            engine = nc.gpsimd if r == 0 else nc.vector
-            engine.tensor_tensor(result[:], old_tiles[r][:, lo:hi], placed[r][:, lo:hi], ADD)
+            for engine, a, b in shares:
+                engine.tensor_tensor(result[:, a - lo : b - lo], old_tiles[r][:, a:b], placed[r][:, a:b], ADD)
             nc.sync.dma_start(out=out[r * P : (r + 1) * P, lo:hi], in_=result[:])
+
+        for r in range(ROW_TILES):
+            place_largest(r)
+        add_and_store(0, [(nc.gpsimd, 0, 256)])
+        add_and_store(0, [(nc.gpsimd, 256, 384), (nc.vector, 384, M)])
+        for r in range(1, ROW_TILES):
+            add_and_store(r, [(nc.vector, 0, M // 2)])
+            add_and_store(r, [(nc.vector, M // 2, M)])

@@ -43,8 +43,8 @@ def tile_attend_tab_plain_runsput_kernel(tc, keys_words, keys_scales, notes, old
 
         notes_by_plane = notes.rearrange("(p t) u -> t p u", t=PACK)
         nc.sync.dma_start(note_list[:], offs2)
-        nc.sync.dma_start(key_list[:], offs)
         nc.sync.dma_start(out=planes[0][:], in_=notes_by_plane[0])
+        nc.sync.dma_start(key_list[:], offs)
         for q in range(4):
             nc.sync.dma_start(
                 out=pool_scales[q:P:32, :].bitcast(I32),
@@ -58,8 +58,7 @@ def tile_attend_tab_plain_runsput_kernel(tc, keys_words, keys_scales, notes, old
             nc.sync.dma_start(out=old_tiles[r][:], in_=old[r * P : (r + 1) * P, :])
 
         for r in range(ROW_TILES):
-            engine = nc.vector if r < 2 else nc.gpsimd
-            engine.memset(placed[r][:], 0.0)
+            nc.vector.memset(placed[r][:], 0.0)
 
         picked = sb.tile([P, PACK, J], BF16, name="picked")
         key_scales = sb.tile([P, I], U8, name="key_scales", align_bytes=64)
@@ -98,36 +97,43 @@ def tile_attend_tab_plain_runsput_kernel(tc, keys_words, keys_scales, notes, old
         gather_notes(nc.vector, 1, 0, J)
         gather_notes(nc.vector, 2, 0, half)
         gather_notes(nc.scalar, 2, half, J)
-        gather_notes(nc.vector, 3, 0, 320)
+        gather_notes(nc.vector, 3, half, 320)
+        gather_notes(nc.vector, 3, 0, half)
         gather_notes(nc.scalar, 3, 320, J)
         weave(nc.scalar, 1, 320, J)
         weave(nc.vector, 1, half, 320)
         weave(nc.vector, 0, 0, half)
         quantise(1)
-        quantise(0)
 
         key_words = sb.tile([P, I], U32, name="key_words", tag="woven1", align_bytes=64)
         word_window = pool_words[:].bitcast(U32)
-        for r in range(ROW_TILES):
+
+        def gather_key_words(r):
             nc.vector.tensor_copy(
                 key_words[:, r * P : (r + 1) * P],
                 word_window.indirect(key_list[:, r * P // 16 : (r + 1) * P // 16]),
             )
+
+        gather_key_words(0)
+        quantise(0)
+        for r in range(1, ROW_TILES):
+            gather_key_words(r)
 
         banks = [psum.tile([P, J], F32, name="bank%d" % r) for r in range(ROW_TILES)]
         largest = [sb.tile([P, N], F32, name="largest%d" % r) for r in range(ROW_TILES)]
 
         def place_largest(r):
             rows = slice(r * P, (r + 1) * P)
-            nc.tensor.matmul_mx(
-                out=banks[r][:],
-                lhsT=key_words[:, rows].bitcast(FP8X4),
-                lhsT_scale=key_scales[:, rows],
-                rhs=note_codes[:].bitcast(FP8X4),
-                rhs_scale=note_scales[:],
-                start=True,
-                stop=True,
-            )
+            for cols in [slice(half, J), slice(0, half)] if r == 0 else [slice(0, J)]:
+                nc.tensor.matmul_mx(
+                    out=banks[r][:, cols],
+                    lhsT=key_words[:, rows].bitcast(FP8X4),
+                    lhsT_scale=key_scales[:, rows],
+                    rhs=note_codes[:, cols].bitcast(FP8X4),
+                    rhs_scale=note_scales[:, cols],
+                    start=True,
+                    stop=True,
+                )
             nc.vector.tensor_reduce(
                 out=largest[r][:],
                 in_=banks[r][:].rearrange("p (n e) -> p n e", e=RUN),
@@ -136,17 +142,16 @@ def tile_attend_tab_plain_runsput_kernel(tc, keys_words, keys_scales, notes, old
             )
             nc.scalar.activation(placed[r][:].indirect(run_list[:]), largest[r][:], COPY)
 
-        def add_and_store(r, shares):
-            lo, hi = shares[0][1], shares[-1][2]
+        def add_and_store(r, lo, hi):
             result = sb.tile([P, hi - lo], F32, name="result%d_%d" % (r, lo))
-            for engine, a, b in shares:
-                engine.tensor_tensor(result[:, a - lo : b - lo], old_tiles[r][:, a:b], placed[r][:, a:b], ADD)
+            nc.vector.tensor_tensor(result[:], old_tiles[r][:, lo:hi], placed[r][:, lo:hi], ADD)
             nc.sync.dma_start(out=out[r * P : (r + 1) * P, lo:hi], in_=result[:])
 
-        for r in range(ROW_TILES):
+        for r in range(ROW_TILES - 1):
             place_largest(r)
-        add_and_store(0, [(nc.gpsimd, 0, 256)])
-        add_and_store(0, [(nc.gpsimd, 256, 384), (nc.vector, 384, M)])
-        for r in range(1, ROW_TILES):
-            add_and_store(r, [(nc.vector, 0, M // 2)])
-            add_and_store(r, [(nc.vector, M // 2, M)])
+        add_and_store(0, 0, M)
+        place_largest(ROW_TILES - 1)
+        add_and_store(1, 0, M)
+        add_and_store(2, 0, M)
+        add_and_store(3, 0, M // 2)
+        add_and_store(3, M // 2, M)

@@ -60,7 +60,7 @@ def tile_attend_tab_plain_runsput_kernel(tc, keys_words, keys_scales, notes, old
         for r in range(ROW_TILES):
             nc.vector.memset(placed[r][:], 0.0)
 
-        picked = sb.tile([P, PACK, J], BF16, name="picked")
+        picked = sb.tile([P, PACK, J], BF16, name="picked", tag="picked", align_bytes=64)
         key_scales = sb.tile([P, I], U8, name="key_scales", align_bytes=64)
 
         def gather_notes(engine, t, lo, hi):
@@ -71,7 +71,7 @@ def tile_attend_tab_plain_runsput_kernel(tc, keys_words, keys_scales, notes, old
                 nc.scalar.activation(picked[:, t, lo:hi], window, COPY)
 
         half = J // 2
-        woven = [sb.tile([P, half, PACK], BF16, name="woven%d" % h, tag="woven%d" % h, align_bytes=64) for h in range(2)]
+        woven = [sb.tile([P, half, PACK], BF16, name="woven%d" % h, align_bytes=64) for h in range(2)]
 
         def weave(engine, h, lo, hi):
             dst = woven[h][:, lo - h * half : hi - h * half, :].rearrange("p (c i) t -> p c t i", i=4)
@@ -105,7 +105,7 @@ def tile_attend_tab_plain_runsput_kernel(tc, keys_words, keys_scales, notes, old
         weave(nc.vector, 0, 0, half)
         quantise(1)
 
-        key_words = sb.tile([P, I], U32, name="key_words", tag="woven1", align_bytes=64)
+        key_words = sb.tile([P, I], U32, name="key_words", tag="picked", align_bytes=64)
         word_window = pool_words[:].bitcast(U32)
 
         def gather_key_words(r):
@@ -142,16 +142,16 @@ def tile_attend_tab_plain_runsput_kernel(tc, keys_words, keys_scales, notes, old
             )
             nc.scalar.activation(placed[r][:].indirect(run_list[:]), largest[r][:], COPY)
 
-        def add_and_store(r, lo, hi):
+        def add_and_store(engine, r, lo, hi):
             result = sb.tile([P, hi - lo], F32, name="result%d_%d" % (r, lo))
-            nc.vector.tensor_tensor(result[:], old_tiles[r][:, lo:hi], placed[r][:, lo:hi], ADD)
+            engine.tensor_tensor(result[:], old_tiles[r][:, lo:hi], placed[r][:, lo:hi], ADD)
             nc.sync.dma_start(out=out[r * P : (r + 1) * P, lo:hi], in_=result[:])
 
-        for r in range(ROW_TILES - 1):
+        for r in range(ROW_TILES):
             place_largest(r)
-        add_and_store(0, 0, M)
-        place_largest(ROW_TILES - 1)
-        add_and_store(1, 0, M)
-        add_and_store(2, 0, M)
-        add_and_store(3, 0, M // 2)
-        add_and_store(3, M // 2, M)
+        add_and_store(nc.gpsimd, 0, 0, M // 2)
+        add_and_store(nc.vector, 0, M // 2, M)
+        add_and_store(nc.vector, 1, 0, M)
+        add_and_store(nc.vector, 2, 0, M)
+        add_and_store(nc.vector, 3, 0, M // 2)
+        add_and_store(nc.vector, 3, M // 2, M)

from contextlib import ExitStack

import concourse.mybir as mybir

F32 = mybir.dt.float32
BF16 = mybir.dt.bfloat16
I32 = mybir.dt.int32
U32 = mybir.dt.uint32
U16 = mybir.dt.uint16
U8 = mybir.dt.uint8
FP8X4 = mybir.dt.float8_e4m3fn_x4
COPY = mybir.ActivationFunctionType.Copy
ADD = mybir.AluOpType.add
MAX = mybir.AluOpType.max
AXIS_X = mybir.AxisListType.X

P = 128
D, T, I, J, U, M, N = 512, 2048, 512, 512, 1024, 512, 64
PACK = 4
RUN = J // N
ROW_TILES = I // P
FLOPS = 2 * D * I * J


def tile_attend_tab_plain_runsput_kernel(tc, keys_words, keys_scales, notes, old, offs, offs2, offs3, out):
    nc = tc.nc
    with ExitStack() as ctx:
        lists = ctx.enter_context(tc.tile_pool(name="lists", bufs=1))
        sb = ctx.enter_context(tc.tile_pool(name="sb", bufs=1))
        psum = ctx.enter_context(tc.psum_pool(name="psum", bufs=1))

        key_list = lists.tile([P, I // 16], U16, name="key_list")
        note_list = lists.tile([P, J // 16], U16, name="note_list")
        run_list = lists.tile([P, N // 16], U16, name="run_list")

        planes = [sb.tile([P, U], F32, name="plane%d" % t) for t in range(PACK)]
        pool_words = sb.tile([P, T], I32, name="pool_words")
        pool_scales = sb.tile([P, T], U8, name="pool_scales")
        old_tiles = [sb.tile([P, M], F32, name="old%d" % r) for r in range(ROW_TILES)]
        placed = [sb.tile([P, M], F32, name="placed%d" % r) for r in range(ROW_TILES)]

        nc.vector.memset(pool_scales[:].bitcast(I32), 0)

        notes_by_plane = notes.rearrange("(p t) u -> t p u", t=PACK)
        nc.sync.dma_start(note_list[:], offs2)
        nc.sync.dma_start(out=planes[0][:], in_=notes_by_plane[0])
        nc.sync.dma_start(key_list[:], offs)
        for q in range(4):
            nc.sync.dma_start(
                out=pool_scales[q:P:32, :].bitcast(I32),
                in_=keys_scales[0, q:16:4, :].bitcast(I32),
            )
        for t in range(1, PACK):
            nc.sync.dma_start(out=planes[t][:], in_=notes_by_plane[t])
        nc.sync.dma_start(out=pool_words[:], in_=keys_words[0].rearrange("p c r -> p (c r)").bitcast(I32))
        nc.sync.dma_start(run_list[:], offs3)
        for r in range(ROW_TILES):
            nc.sync.dma_start(out=old_tiles[r][:], in_=old[r * P : (r + 1) * P, :])

        for r in range(ROW_TILES):
            nc.vector.memset(placed[r][:], 0.0)

        picked = sb.tile([P, PACK, J], BF16, name="picked", tag="picked", align_bytes=64)
        key_scales = sb.tile([P, I], U8, name="key_scales", align_bytes=64)

        def gather_notes(engine, t, lo, hi):
            window = planes[t][:].indirect(note_list[:, lo // 16 : hi // 16])
            if engine is nc.vector:
                nc.vector.tensor_copy(picked[:, t, lo:hi], window)
            else:
                nc.scalar.activation(picked[:, t, lo:hi], window, COPY)

        half = J // 2
        woven = [sb.tile([P, half, PACK], BF16, name="woven%d" % h, align_bytes=64) for h in range(2)]

        def weave(engine, h, lo, hi):
            dst = woven[h][:, lo - h * half : hi - h * half, :].rearrange("p (c i) t -> p c t i", i=4)
            src = picked[:, :, lo:hi].rearrange("p t (c i) -> p c t i", i=4)
            if engine is nc.vector:
                nc.vector.tensor_copy(dst, src)
            else:
                nc.scalar.copy(dst, src)

        note_codes = sb.tile([P, J], U32, name="note_codes", align_bytes=64)
        note_scales = sb.tile([P, J], U8, name="note_scales", align_bytes=64)

        def quantise(h):
            cols = slice(h * half, (h + 1) * half)
            nc.vector.quantize_mx(
                out=note_codes[:, cols].bitcast(FP8X4),
                scales=note_scales[:, cols],
                in_=woven[h][:].rearrange("p c t -> p (c t)"),
            )

        nc.vector.tensor_copy(key_scales[:], pool_scales[:].indirect(key_list[:]))
        gather_notes(nc.scalar, 0, 0, J)
        gather_notes(nc.vector, 1, 0, J)
        gather_notes(nc.vector, 2, 0, half)
        gather_notes(nc.scalar, 2, half, J)
        gather_notes(nc.vector, 3, half, 320)
        gather_notes(nc.vector, 3, 0, half)
        gather_notes(nc.scalar, 3, 320, J)
        weave(nc.scalar, 1, 320, J)
        weave(nc.vector, 1, half, 320)
        weave(nc.vector, 0, 0, half)
        quantise(1)

        key_words = sb.tile([P, I], U32, name="key_words", tag="picked", align_bytes=64)
        word_window = pool_words[:].bitcast(U32)

        def gather_key_words(r):
            nc.vector.tensor_copy(
                key_words[:, r * P : (r + 1) * P],
                word_window.indirect(key_list[:, r * P // 16 : (r + 1) * P // 16]),
            )

        gather_key_words(0)
        quantise(0)
        for r in range(1, ROW_TILES):
            gather_key_words(r)

        banks = [psum.tile([P, J], F32, name="bank%d" % r) for r in range(ROW_TILES)]
        largest = [sb.tile([P, N], F32, name="largest%d" % r) for r in range(ROW_TILES)]

        def place_largest(r):
            rows = slice(r * P, (r + 1) * P)
            for cols in [slice(half, J), slice(0, half)] if r == 0 else [slice(0, J)]:
                nc.tensor.matmul_mx(
                    out=banks[r][:, cols],
                    lhsT=key_words[:, rows].bitcast(FP8X4),
                    lhsT_scale=key_scales[:, rows],
                    rhs=note_codes[:, cols].bitcast(FP8X4),
                    rhs_scale=note_scales[:, cols],
                    start=True,
                    stop=True,
                )
            nc.vector.tensor_reduce(
                out=largest[r][:],
                in_=banks[r][:].rearrange("p (n e) -> p n e", e=RUN),
                axis=AXIS_X,
                op=MAX,
            )
            nc.scalar.activation(placed[r][:].indirect(run_list[:]), largest[r][:], COPY)

        def add_and_store(engine, r, lo, hi):
            result = sb.tile([P, hi - lo], F32, name="result%d_%d" % (r, lo))
            engine.tensor_tensor(result[:], old_tiles[r][:, lo:hi], placed[r][:, lo:hi], ADD)
            nc.sync.dma_start(out=out[r * P : (r + 1) * P, lo:hi], in_=result[:])

        for r in range(ROW_TILES):
            place_largest(r)
        add_and_store(nc.gpsimd, 0, 0, M // 2)
        add_and_store(nc.vector, 0, M // 2, M)
        add_and_store(nc.vector, 1, 0, M)
        add_and_store(nc.vector, 2, 0, M)
        add_and_store(nc.vector, 3, 0, M // 2)
        add_and_store(nc.vector, 3, M // 2, M)
